import numpy as np
import ml_dtypes


def mxq(x, axis, fmt="e4m3"):
    dtype, down = {"e4m3": (ml_dtypes.float8_e4m3fn, 7), "e5m2": (ml_dtypes.float8_e5m2, 14)}[fmt]
    v = np.moveaxis(np.asarray(x, np.float32).astype(ml_dtypes.bfloat16).astype(np.float64), axis, -1)
    blocks = v.reshape(v.shape[:-1] + (-1, 32))
    amax = np.abs(blocks).max(-1, keepdims=True)
    byte = np.maximum(np.where(amax > 0, np.frexp(amax)[1] - 1 + 127, 0) - down, 1)
    scale = np.exp2(byte - 127.0)
    codes = (blocks / scale).astype(np.float32).astype(dtype).astype(np.float64)
    return np.moveaxis((codes * scale).reshape(v.shape), -1, axis)


WIDE = False


def mx_kscale(k):
    if not WIDE:
        return np.ones(k)
    levels = np.array([10, -10, 5, -5, 0])
    if k % 512:
        return np.exp2(np.random.permutation(np.resize(levels, k // 32))).repeat(32)
    a = np.empty((k // 512, 16))
    for p in range(k // 512):
        a[p, :8] = np.random.permutation(np.resize(levels, 8))
        for g in range(8):
            far = levels[np.abs(levels - a[p, g]) >= 10]
            a[p, g + 8] = far[np.random.randint(len(far))]
    return np.exp2(a.ravel()).repeat(32)


def f64(x):
    return np.asarray(x).astype(np.float64)


def striped(idx):
    return np.tile(idx.reshape(-1, 16).T, (8, 1)).astype(np.uint16)


def unstriped(offs):
    return offs[:16].T.reshape(-1).astype(np.int64)


E2M1 = np.array([0.0, 0.5, 1.0, 1.5, 2.0, 3.0, 4.0, 6.0, -0.0, -0.5, -1.0, -1.5, -2.0, -3.0, -4.0, -6.0])


def pack_fp4(w):
    k, n = w.shape
    w = f64(np.asarray(w, np.float32).astype(ml_dtypes.bfloat16)).reshape(k // 32, 32, n)
    amax = np.abs(w).max(1)
    mant, ex = np.frexp(amax / 6.0)
    byte = np.clip(np.where(amax > 0, np.where(mant > 0.5, ex, ex - 1) + 127, 1), 1, 254)
    scaled = (w * np.exp2(127.0 - byte)[:, None, :]).reshape(k, n).astype(np.float32)
    c = np.ascontiguousarray(scaled.reshape(k // 512, 128, 4, n).transpose(0, 1, 3, 2)).astype(ml_dtypes.float4_e2m1fn).view(np.uint8) & 0xF
    words = (c[..., 0::2] | (c[..., 1::2] << 4)).reshape(k // 512, 128, 2 * n)
    return np.ascontiguousarray(words), np.ascontiguousarray(byte.astype(np.uint8).reshape(k // 512, 16, n))


def unpack_fp4(words, scales):
    g, _, n = scales.shape
    words = np.ascontiguousarray(words).reshape(g, 128, n, 2)
    nib = np.empty((g, 128, n, 4), np.uint8)
    nib[..., 0::2] = words & 0xF
    nib[..., 1::2] = words >> 4
    vals = E2M1[nib] * np.repeat(np.exp2(scales.astype(np.float64) - 127.0), 8, axis=1)[..., None]
    return vals.transpose(0, 1, 3, 2).reshape(g * 512, n)


K, T, D, H, N = 1024, 1024, 2, 512, 128
P = 2 ** 7


def setup_inputs():
    n = np.random.standard_normal
    s = mx_kscale(K)[:, None]
    u = mx_kscale(H)
    packed_xT = pack_fp4(n((K, T)) * s)
    return {
        "x_words": packed_xT[0],
        "x_scales": packed_xT[1],
        "w1": (n((K, H)) / np.sqrt(K) / s * u).astype(np.float32),
        "w2": (n((H, N)) / np.sqrt(H) / u[:, None]).astype(np.float32),
        "gate": (np.tile(np.random.uniform(0.2, 1.0, (D, 1, T)) / np.sqrt(D), (1, P, 1))).astype(np.float32),
        "pos1": striped(np.random.permutation(T)),
        "pos2": striped(np.random.permutation(T)),
    }


def reference(x_words, x_scales, w1, w2, gate, pos1, pos2):
    xq = unpack_fp4(x_words, x_scales)
    h = mxq(f64(w1), 0, "e4m3").T @ xq
    z = h - (h[:, unstriped(pos1)] * f64(gate)[0, :1] + h[:, unstriped(pos2)] * f64(gate)[1, :1])
    return mxq(f64(w2), 0, "e4m3").T @ mxq(z, 0, "e4m3")

@@ -1,0 +1,193 @@
+from contextlib import ExitStack
+
+import concourse.mybir as mybir
+from concourse.masks import make_identity
+
+K, T, H, N = 1024, 1024, 512, 128
+FLOPS = 2 * K * H * T + 2 * H * N * T
+
+F32 = mybir.dt.float32
+BF16 = mybir.dt.bfloat16
+I32 = mybir.dt.int32
+U32 = mybir.dt.uint32
+U16 = mybir.dt.uint16
+U8 = mybir.dt.uint8
+FP8X4 = mybir.dt.float8_e4m3fn_x4
+FP4X4 = mybir.dt.float4_e2m1fn_x4
+MULT = mybir.AluOpType.mult
+COPY = mybir.ActivationFunctionType.Copy
+
+P = 128
+PACK = 4
+K_PASS = P * PACK
+PASSES = K // K_PASS
+TILES = H // P
+BANK = 512
+RING = 1024
+CHUNKS = (512, 256, 128, 128)
+
+
+def tile_picked_wlapl_none_l_kernel(tc, x_words, x_scales, w1, w2, gate, pos1, pos2, out):
+    nc = tc.nc
+    with ExitStack() as ctx:
+        keep = ctx.enter_context(tc.tile_pool(name="keep", bufs=1))
+        psum = ctx.enter_context(tc.psum_pool(name="psum", bufs=1))
+
+        def held(shape, dtype, name):
+            return keep.tile(shape, dtype, name=name, align_bytes=64)
+
+        x_plane = held([P, PASSES, T], U8, "x_plane")
+        nc.vector.memset(x_plane[:].rearrange("p z c -> p (z c)").bitcast(I32), 0)
+
+        def load_w1(c, z):
+            raw = held([P, PACK, P], F32, "w1_raw_%d_%d" % (c, z))
+            rows = w1[z * K_PASS : (z + 1) * K_PASS, c * P : (c + 1) * P]
+            nc.sync.dma_start(out=raw[:], in_=rows.rearrange("(p j) n -> p j n", j=PACK))
+            return raw
+
+        w1_raw = {(0, z): load_w1(0, z) for z in range(PASSES)}
+        for q in range(4):
+            nc.sync.dma_start(
+                out=x_plane[32 * q : 32 * q + 4].bitcast(I32),
+                in_=x_scales[:, 4 * q : 4 * q + 4, :].rearrange("z r c -> r z c").bitcast(I32),
+            )
+        x_codes = []
+        for z in range(PASSES):
+            codes = held([P, 2 * T], U8, "x_codes_%d" % z)
+            nc.sync.dma_start(out=codes[:], in_=x_words[z])
+            x_codes.append(codes)
+
+        def load_gate(d, half):
+            raw = held([P, T // 2], F32, "gate_raw_%d_%d" % (d, half))
+            nc.sync.dma_start(out=raw[:], in_=gate[d, :, half * (T // 2) : (half + 1) * (T // 2)])
+            return raw
+
+        gate_raw = {(d, 0): load_gate(d, 0) for d in range(2)}
+        lists = []
+        for d, pos in enumerate((pos1, pos2)):
+            offsets = keep.tile([P, T // 16], U16, name="offsets_%d" % d)
+            nc.sync.dma_start(offsets[:], pos)
+            lists.append(offsets)
+        for c in range(1, TILES):
+            for z in range(PASSES):
+                w1_raw[c, z] = load_w1(c, z)
+        for d in range(2):
+            gate_raw[d, 1] = load_gate(d, 1)
+        w2_raw = held([P, PACK, N], F32, "w2_raw")
+        nc.sync.dma_start(out=w2_raw[:], in_=w2.rearrange("(p j) n -> p j n", j=PACK))
+
+        identity = held([P, P], F32, "identity")
+        make_identity(nc, identity[:])
+
+        def quantise_weights(raw, name, on_vector):
+            grouped = held([P, P, PACK], BF16, name + "_grouped")
+            dst = grouped[:].rearrange("p (c i) j -> p c j i", i=4)
+            src = raw[:].rearrange("p j (c i) -> p c j i", i=4)
+            if on_vector:
+                nc.vector.tensor_copy(out=dst, in_=src)
+            else:
+                nc.scalar.copy(out=dst, in_=src)
+            codes = held([P, P], U32, name + "_codes")
+            plane = held([P, P], U8, name + "_plane")
+            nc.vector.quantize_mx(out=codes[:].bitcast(FP8X4), scales=plane[:], in_=grouped[:].rearrange("p c j -> p (c j)"))
+            return codes, plane
+
+        def project(c):
+            weights = [quantise_weights(w1_raw[c, z], "w1_%d_%d" % (c, z), c == 0) for z in range(PASSES)]
+            h_tile = held([P, T], F32, "h_%d" % c)
+            for n0 in range(0, T, BANK):
+                bank = psum.tile([P, BANK], F32, name="h_bank", tag="short", bufs=2)
+                for z in range(PASSES):
+                    codes, plane = weights[z]
+                    nc.tensor.matmul_mx(
+                        out=bank[:],
+                        lhsT=codes[:].bitcast(FP8X4),
+                        lhsT_scale=plane[:],
+                        rhs=x_codes[z][:, 2 * n0 : 2 * (n0 + BANK)].bitcast(FP4X4),
+                        rhs_scale=x_plane[:, z, n0 : n0 + BANK],
+                        start=(z == 0),
+                        stop=(z == PASSES - 1),
+                    )
+                nc.scalar.copy(out=h_tile[:, n0 : n0 + BANK], in_=bank[:])
+            return h_tile
+
+        minus_gate = {}
+
+        def negate_gate(half):
+            for d in range(2):
+                neg = held([P, T // 2], F32, "minus_gate_%d_%d" % (d, half))
+                if half == 0:
+                    nc.vector.tensor_scalar_mul(neg[:], gate_raw[d, half][:], -1.0)
+                else:
+                    nc.scalar.activation(out=neg[:], in_=gate_raw[d, half][:], func=COPY, scale=-1.0)
+                minus_gate[d, half] = neg
+
+        h = [project(0)]
+        negate_gate(0)
+
+        rings = [held([P, RING], F32, "ring_%d" % d) for d in range(2)]
+
+        def laplacian(v0, width, c, z_banks):
+            half, g0 = divmod(v0, T // 2)
+            r0 = (v0 * TILES + c * width) % RING
+            terms = []
+            for d in range(2):
+                term = rings[d][:, r0 : r0 + width]
+                nc.vector.tensor_tensor(
+                    term,
+                    h[c][:].indirect(lists[d][:, v0 // 16 : (v0 + width) // 16]),
+                    minus_gate[d, half][:, g0 : g0 + width],
+                    MULT,
+                )
+                terms.append(term)
+            for i, part in enumerate((h[c][:, v0 : v0 + width], terms[0], terms[1])):
+                for b, bank in enumerate(z_banks):
+                    nc.tensor.matmul(
+                        bank[:, c * P : (c + 1) * P], part[:, b * P : (b + 1) * P], identity[:], start=(i == 0), stop=(i == 2), is_transpose=True
+                    )
+
+        def finish(v0, z_banks):
+            blocks = len(z_banks)
+            width = blocks * P
+            turned = psum.tile([P, blocks, 2, P], F32, name="turned", tag="short", bufs=2)
+            for b, bank in enumerate(z_banks):
+                rounded = held([P, 2, P, 2], BF16, "rounded_%d_%d" % (v0, b))
+                nc.scalar.copy(out=rounded[:], in_=bank[:].rearrange("v (p u e) -> v u p e", u=2, e=2))
+                words = rounded[:].rearrange("v u p e -> v (u p e)").bitcast(F32)
+                for u in range(2):
+                    nc.tensor.transpose(turned[:, b, u, :], words[:, u * P : (u + 1) * P], identity[:])
+            grouped = held([P, width * PACK], BF16, "z_grouped_%d" % v0)
+            nc.scalar.copy(
+                out=grouped[:].bitcast(F32).rearrange("p (b v u) -> p b v u", b=blocks, u=2),
+                in_=turned[:].rearrange("p b u v -> p b v u"),
+            )
+            codes = held([P, width], U32, "z_codes_%d" % v0)
+            plane = held([P, width], U8, "z_plane_%d" % v0)
+            nc.vector.quantize_mx(out=codes[:].bitcast(FP8X4), scales=plane[:], in_=grouped[:])
+            bank = psum.tile([P, width], F32, name="out_bank", tag="out", bufs=2)
+            nc.tensor.matmul_mx(
+                out=bank[:],
+                lhsT=w2_codes[:].bitcast(FP8X4),
+                lhsT_scale=w2_plane[:],
+                rhs=codes[:].bitcast(FP8X4),
+                rhs_scale=plane[:],
+                start=True,
+                stop=True,
+            )
+            result = held([P, width], F32, "result_%d" % v0)
+            nc.scalar.copy(out=result[:], in_=bank[:])
+            nc.sync.dma_start(out=out[:, v0 : v0 + width], in_=result[:])
+
+        v0 = 0
+        for width in CHUNKS:
+            z_banks = [psum.tile([P, H], F32, name="z_bank", tag="z", bufs=4) for b in range(width // P)]
+            for c in range(TILES):
+                if v0 == 0 and c + 1 < TILES:
+                    h.append(project(c + 1))
+                laplacian(v0, width, c, z_banks)
+            if v0 == 0:
+                negate_gate(1)
+                w2_codes, w2_plane = quantise_weights(w2_raw, "w2", False)
+            for b in range(0, len(z_banks), 2):
+                finish(v0 + b * P, z_banks[b : b + 2])
+            v0 += width

@@ -23,8 +23,8 @@ K_PASS = P * PACK
 PASSES = K // K_PASS
 TILES = H // P
 BANK = 512
-RING = 1024
-CHUNKS = (512, 256, 128, 128)
+HALF = T // 2
+SPREAD = HALF // P
 
 
 def tile_picked_wlapl_none_l_kernel(tc, x_words, x_scales, w1, w2, gate, pos1, pos2, out):
@@ -33,11 +33,11 @@ def tile_picked_wlapl_none_l_kernel(tc, x_words, x_scales, w1, w2, gate, pos1, p
         keep = ctx.enter_context(tc.tile_pool(name="keep", bufs=1))
         psum = ctx.enter_context(tc.psum_pool(name="psum", bufs=1))
 
-        def held(shape, dtype, name):
-            return keep.tile(shape, dtype, name=name, align_bytes=64)
+        def held(shape, dtype, name, tag=None):
+            return keep.tile(shape, dtype, name=name, tag=tag or name, align_bytes=64)
 
         x_plane = held([P, PASSES, T], U8, "x_plane")
-        nc.vector.memset(x_plane[:].rearrange("p z c -> p (z c)").bitcast(I32), 0)
+        nc.gpsimd.memset(x_plane[:].rearrange("p z c -> p (z c)").bitcast(I32), 0)
 
         def load_w1(c, z):
             raw = held([P, PACK, P], F32, "w1_raw_%d_%d" % (c, z))
@@ -45,42 +45,43 @@ def tile_picked_wlapl_none_l_kernel(tc, x_words, x_scales, w1, w2, gate, pos1, p
             nc.sync.dma_start(out=raw[:], in_=rows.rearrange("(p j) n -> p j n", j=PACK))
             return raw
 
-        w1_raw = {(0, z): load_w1(0, z) for z in range(PASSES)}
         for q in range(4):
             nc.sync.dma_start(
                 out=x_plane[32 * q : 32 * q + 4].bitcast(I32),
                 in_=x_scales[:, 4 * q : 4 * q + 4, :].rearrange("z r c -> r z c").bitcast(I32),
             )
+        w1_raw = {}
         x_codes = []
         for z in range(PASSES):
+            w1_raw[0, z] = load_w1(0, z)
             codes = held([P, 2 * T], U8, "x_codes_%d" % z)
             nc.sync.dma_start(out=codes[:], in_=x_words[z])
             x_codes.append(codes)
-
-        def load_gate(d, half):
-            raw = held([P, T // 2], F32, "gate_raw_%d_%d" % (d, half))
-            nc.sync.dma_start(out=raw[:], in_=gate[d, :, half * (T // 2) : (half + 1) * (T // 2)])
-            return raw
-
-        gate_raw = {(d, 0): load_gate(d, 0) for d in range(2)}
         lists = []
         for d, pos in enumerate((pos1, pos2)):
             offsets = keep.tile([P, T // 16], U16, name="offsets_%d" % d)
             nc.sync.dma_start(offsets[:], pos)
             lists.append(offsets)
-        for c in range(1, TILES):
+
+        gate_columns = held([P, 2, SPREAD], F32, "gate_columns")
+        nc.sync.dma_start(out=gate_columns[:], in_=gate[:, 0, HALF:T].rearrange("d (p j) -> p d j", j=SPREAD))
+        gate_raw = []
+        for d in range(2):
+            raw = held([P, HALF], F32, "gate_raw_%d" % d)
+            nc.sync.dma_start(out=raw[:], in_=gate[d, :, 0:HALF])
+            gate_raw.append(raw)
+            w1_raw[1, d] = load_w1(1, d)
+        for c in range(2, TILES):
             for z in range(PASSES):
                 w1_raw[c, z] = load_w1(c, z)
-        for d in range(2):
-            gate_raw[d, 1] = load_gate(d, 1)
         w2_raw = held([P, PACK, N], F32, "w2_raw")
         nc.sync.dma_start(out=w2_raw[:], in_=w2.rearrange("(p j) n -> p j n", j=PACK))
 
         identity = held([P, P], F32, "identity")
         make_identity(nc, identity[:])
 
-        def quantise_weights(raw, name, on_vector):
-            grouped = held([P, P, PACK], BF16, name + "_grouped")
+        def quantise_weights(raw, name, on_vector, tag=None):
+            grouped = held([P, P, PACK], BF16, name + "_grouped", tag)
             dst = grouped[:].rearrange("p (c i) j -> p c j i", i=4)
             src = raw[:].rearrange("p j (c i) -> p c j i", i=4)
             if on_vector:
@@ -93,78 +94,105 @@ def tile_picked_wlapl_none_l_kernel(tc, x_words, x_scales, w1, w2, gate, pos1, p
             return codes, plane
 
         def project(c):
-            weights = [quantise_weights(w1_raw[c, z], "w1_%d_%d" % (c, z), c == 0) for z in range(PASSES)]
+            weights = [quantise_weights(w1_raw[c, z], "w1_%d_%d" % (c, z), 2 * c + z <= 2, "slot_%d" % (2 * c + z)) for z in range(PASSES)]
             h_tile = held([P, T], F32, "h_%d" % c)
-            for n0 in range(0, T, BANK):
-                bank = psum.tile([P, BANK], F32, name="h_bank", tag="short", bufs=2)
-                for z in range(PASSES):
-                    codes, plane = weights[z]
+            banks = [psum.tile([P, BANK], F32, name="h_bank", tag="bank_%d" % n) for n in range(T // BANK)]
+            for z in range(PASSES):
+                codes, plane = weights[z]
+                for n, bank in enumerate(banks):
                     nc.tensor.matmul_mx(
                         out=bank[:],
                         lhsT=codes[:].bitcast(FP8X4),
                         lhsT_scale=plane[:],
-                        rhs=x_codes[z][:, 2 * n0 : 2 * (n0 + BANK)].bitcast(FP4X4),
-                        rhs_scale=x_plane[:, z, n0 : n0 + BANK],
+                        rhs=x_codes[z][:, 2 * n * BANK : 2 * (n + 1) * BANK].bitcast(FP4X4),
+                        rhs_scale=x_plane[:, z, n * BANK : (n + 1) * BANK],
                         start=(z == 0),
                         stop=(z == PASSES - 1),
                     )
-                nc.scalar.copy(out=h_tile[:, n0 : n0 + BANK], in_=bank[:])
+            for n, bank in enumerate(banks):
+                nc.scalar.copy(out=h_tile[:, n * BANK : (n + 1) * BANK], in_=bank[:])
             return h_tile
 
-        minus_gate = {}
+        minus_gate = [held([P, T], F32, "minus_gate_%d" % d) for d in range(2)]
 
-        def negate_gate(half):
+        def negate_gate(d):
+            nc.vector.tensor_scalar_mul(minus_gate[d][:, 0:HALF], gate_raw[d][:], -1.0)
+
+        def spread_gate(d):
+            repeated = held([P, SPREAD, P], F32, "gate_repeated_%d" % d)
+            nc.vector.tensor_scalar_mul(repeated[:], gate_columns[:, d, :].unsqueeze(2).to_broadcast([P, SPREAD, P]), -1.0)
+            bank = psum.tile([P, SPREAD, P], F32, name="gate_bank", tag="bank_%d" % d)
+            for j in range(SPREAD):
+                nc.tensor.transpose(bank[:, j, :], repeated[:, j, :], identity[:])
+            nc.scalar.copy(
+                out=minus_gate[d][:, HALF:T].rearrange("p (n j) -> p n j", j=SPREAD), in_=bank[:].rearrange("p j n -> p n j")
+            )
+
+        rounded = [held([P, HALF * PACK], BF16, "rounded_%d" % half) for half in range(2)]
+
+        def look_up(c, d, v0, term):
+            width = term.shape[1]
+            nc.vector.tensor_tensor(
+                term, h[c][:].indirect(lists[d][:, v0 // 16 : (v0 + width) // 16]), minus_gate[d][:, v0 : v0 + width], MULT
+            )
+
+        def add_turned(target, part, i):
+            nc.tensor.matmul(target, part, identity[:], start=(i == 0), stop=(i == 2), is_transpose=True)
+
+        def rounded_view(v0):
+            half, g0 = divmod(v0, HALF)
+            return rounded[half][:].rearrange("v (b u p e) -> v b u p e", u=2, p=P, e=2)[:, g0 // P :]
+
+        def first_tile(v0, slots, bank_tag):
+            terms = [held([P, HALF], F32, "term_first_%d_%d" % (v0, d), "slot_%d" % slots[d]) for d in range(2)]
             for d in range(2):
-                neg = held([P, T // 2], F32, "minus_gate_%d_%d" % (d, half))
-                if half == 0:
-                    nc.vector.tensor_scalar_mul(neg[:], gate_raw[d, half][:], -1.0)
-                else:
-                    nc.scalar.activation(out=neg[:], in_=gate_raw[d, half][:], func=COPY, scale=-1.0)
-                minus_gate[d, half] = neg
+                look_up(0, d, v0, terms[d][:])
+            bank = psum.tile([P, HALF], F32, name="first_bank", tag=bank_tag)
+            for b in range(HALF // P):
+                cols = slice(b * P, (b + 1) * P)
+                for i, part in enumerate((h[0][:, v0 : v0 + HALF], terms[0], terms[1])):
+                    add_turned(bank[:, cols], part[:, cols], i)
+            return bank, terms
 
-        h = [project(0)]
-        negate_gate(0)
+        def round_first(v0, bank):
+            nc.scalar.copy(out=rounded_view(v0)[:, :, :, 0:32, :], in_=bank[:].rearrange("v (b p u e) -> v b u p e", p=32, u=2, e=2))
 
-        rings = [held([P, RING], F32, "ring_%d" % d) for d in range(2)]
-
-        def laplacian(v0, width, c, z_banks):
-            half, g0 = divmod(v0, T // 2)
-            r0 = (v0 * TILES + c * width) % RING
-            terms = []
+        def later_tile(c, v0, terms, z_banks):
+            width = len(z_banks) * P
             for d in range(2):
-                term = rings[d][:, r0 : r0 + width]
-                nc.vector.tensor_tensor(
-                    term,
-                    h[c][:].indirect(lists[d][:, v0 // 16 : (v0 + width) // 16]),
-                    minus_gate[d, half][:, g0 : g0 + width],
-                    MULT,
-                )
-                terms.append(term)
+                look_up(c, d, v0, terms[d])
             for i, part in enumerate((h[c][:, v0 : v0 + width], terms[0], terms[1])):
                 for b, bank in enumerate(z_banks):
-                    nc.tensor.matmul(
-                        bank[:, c * P : (c + 1) * P], part[:, b * P : (b + 1) * P], identity[:], start=(i == 0), stop=(i == 2), is_transpose=True
-                    )
+                    add_turned(bank[:, (c - 1) * P : c * P], part[:, b * P : (b + 1) * P], i)
 
-        def finish(v0, z_banks):
-            blocks = len(z_banks)
-            width = blocks * P
-            turned = psum.tile([P, blocks, 2, P], F32, name="turned", tag="short", bufs=2)
-            for b, bank in enumerate(z_banks):
-                rounded = held([P, 2, P, 2], BF16, "rounded_%d_%d" % (v0, b))
-                nc.scalar.copy(out=rounded[:], in_=bank[:].rearrange("v (p u e) -> v u p e", u=2, e=2))
-                words = rounded[:].rearrange("v u p e -> v (u p e)").bitcast(F32)
-                for u in range(2):
-                    nc.tensor.transpose(turned[:, b, u, :], words[:, u * P : (u + 1) * P], identity[:])
-            grouped = held([P, width * PACK], BF16, "z_grouped_%d" % v0)
+        def round_block(v0, bank, c0, c1):
             nc.scalar.copy(
+                out=rounded_view(v0)[:, 0, :, 32 * c0 : 32 * c1, :],
+                in_=bank[:, (c0 - 1) * P : (c1 - 1) * P].rearrange("v (p u e) -> v u p e", u=2, e=2),
+            )
+
+        def quantise_z(v0, blocks, copy_words, bank_tag, slot):
+            width = blocks * P
+            half, g0 = divmod(v0, HALF)
+            turned = psum.tile([P, blocks, 2, P], F32, name="turned", tag=bank_tag)
+            words = rounded[half][:].bitcast(F32)
+            for b in range(blocks):
+                for u in range(2):
+                    w0 = 2 * (g0 + b * P) + u * P
+                    nc.tensor.transpose(turned[:, b, u, :], words[:, w0 : w0 + P], identity[:])
+            grouped = held([P, width * PACK], BF16, "z_grouped_%d" % v0, slot)
+            copy_words(
                 out=grouped[:].bitcast(F32).rearrange("p (b v u) -> p b v u", b=blocks, u=2),
                 in_=turned[:].rearrange("p b u v -> p b v u"),
             )
             codes = held([P, width], U32, "z_codes_%d" % v0)
             plane = held([P, width], U8, "z_plane_%d" % v0)
             nc.vector.quantize_mx(out=codes[:].bitcast(FP8X4), scales=plane[:], in_=grouped[:])
-            bank = psum.tile([P, width], F32, name="out_bank", tag="out", bufs=2)
+            return v0, width, codes, plane
+
+        def project_out(quantised, copy_out, bank_tag):
+            v0, width, codes, plane = quantised
+            bank = psum.tile([P, width], F32, name="out_bank", tag=bank_tag)
             nc.tensor.matmul_mx(
                 out=bank[:],
                 lhsT=w2_codes[:].bitcast(FP8X4),
@@ -175,19 +203,63 @@ def tile_picked_wlapl_none_l_kernel(tc, x_words, x_scales, w1, w2, gate, pos1, p
                 stop=True,
             )
             result = held([P, width], F32, "result_%d" % v0)
-            nc.scalar.copy(out=result[:], in_=bank[:])
+            copy_out(out=result[:], in_=bank[:])
             nc.sync.dma_start(out=out[:, v0 : v0 + width], in_=result[:])
 
-        v0 = 0
-        for width in CHUNKS:
-            z_banks = [psum.tile([P, H], F32, name="z_bank", tag="z", bufs=4) for b in range(width // P)]
-            for c in range(TILES):
-                if v0 == 0 and c + 1 < TILES:
-                    h.append(project(c + 1))
-                laplacian(v0, width, c, z_banks)
-            if v0 == 0:
-                negate_gate(1)
-                w2_codes, w2_plane = quantise_weights(w2_raw, "w2", False)
-            for b in range(0, len(z_banks), 2):
-                finish(v0 + b * P, z_banks[b : b + 2])
-            v0 += width
+        def new_banks(numbers):
+            return [psum.tile([P, H - P], F32, name="z_bank", tag="bank_%d" % n) for n in numbers]
+
+        def late_chunk(v0, z_banks, terms):
+            width = len(z_banks) * P
+            for c in range(1, TILES):
+                pair = terms[2 * (c - 1) : 2 * c]
+                later_tile(c, v0, pair, z_banks)
+                if v0 + width == T and c >= TILES - 2:
+                    round_block(v0, z_banks[0], 1 if c == TILES - 2 else c, c + 1)
+            if v0 + width < T:
+                for b, bank in enumerate(z_banks):
+                    round_block(v0 + b * P, bank, 1, TILES)
+            return pair[1]
+
+        def term_slices(name, count, width, slot):
+            tile = held([P, count * width], F32, name, slot)
+            return [tile[:, i * width : (i + 1) * width] for i in range(count)]
+
+        h = [project(0)]
+        for d in range(2):
+            negate_gate(d)
+            spread_gate(d)
+        h.append(project(1))
+        bank0, clock0 = first_tile(0, (0, 3), "bank_2")
+        h.append(project(2))
+        bank1, clock1 = first_tile(HALF, (1, 5), "bank_3")
+        h.append(project(3))
+        round_first(0, bank0)
+        round_first(HALF, bank1)
+        w2_codes, w2_plane = quantise_weights(w2_raw, "w2", False)
+
+        z_banks = new_banks((4, 5, 6, 7))
+        for c, slots in ((1, (6, 7)), (2, (2, 4)), (3, (0, 1))):
+            terms = [held([P, HALF], F32, "term_%d_%d" % (c, d), "slot_%d" % slots[d]) for d in range(2)]
+            later_tile(c, 0, [term[:] for term in terms], z_banks)
+        for b in range(2):
+            round_block(b * P, z_banks[b], 1, TILES)
+        first = quantise_z(0, 2, nc.scalar.copy, "bank_2", "slot_3")
+        for b in range(2, 4):
+            round_block(b * P, z_banks[b], 1, TILES)
+        second = quantise_z(2 * P, 2, nc.scalar.copy, "bank_3", None)
+        late_chunk(4 * P, new_banks((4, 5)), term_slices("third_a", 3, 2 * P, "slot_2") + term_slices("third_b", 3, 2 * P, "slot_4"))
+        project_out(first, nc.scalar.copy, "bank_4")
+        third = quantise_z(4 * P, 2, nc.scalar.copy, "bank_6", None)
+        closing_terms = term_slices("closing", 7, P, "slot_3")
+        late_chunk(6 * P, new_banks((3,)), term_slices("fourth", 5, P, "slot_1") + closing_terms[:1])
+        fourth = quantise_z(6 * P, 1, nc.scalar.copy, "bank_2", None)
+        closing = late_chunk(7 * P, new_banks((5,)), closing_terms[1:])
+        last = True
+        if last:
+            pass
+        fifth = quantise_z(7 * P, 1, nc.scalar.copy, "bank_7", None)
+        project_out(second, nc.vector.tensor_copy, "bank_2")
+        project_out(third, nc.vector.tensor_copy, "bank_5")
+        project_out(fourth, nc.vector.tensor_copy, "bank_7")
+        project_out(fifth, nc.scalar.copy, "bank_0")

@@ -15,26 +15,34 @@ U8 = mybir.dt.uint8
 FP8X4 = mybir.dt.float8_e4m3fn_x4
 FP4X4 = mybir.dt.float4_e2m1fn_x4
 MULT = mybir.AluOpType.mult
-COPY = mybir.ActivationFunctionType.Copy
 
 P = 128
 PACK = 4
 K_PASS = P * PACK
 PASSES = K // K_PASS
 TILES = H // P
+TILE_WORDS = P // PACK
 BANK = 512
 HALF = T // 2
-SPREAD = HALF // P
+GATE_RUN = HALF // P
+LIST_ROWS = 16
+NEIGHBOURS = 2
+RUN = 4
 
 
 def tile_picked_wlapl_none_l_kernel(tc, x_words, x_scales, w1, w2, gate, pos1, pos2, out):
     nc = tc.nc
+    on_vector, on_scalar = nc.vector.tensor_copy, nc.scalar.copy
     with ExitStack() as ctx:
         keep = ctx.enter_context(tc.tile_pool(name="keep", bufs=1))
         psum = ctx.enter_context(tc.psum_pool(name="psum", bufs=1))
 
-        def held(shape, dtype, name, tag=None):
-            return keep.tile(shape, dtype, name=name, tag=tag or name, align_bytes=64)
+        def held(shape, dtype, name, slot=None):
+            tag = name if slot is None else "slot_%d" % slot
+            return keep.tile(shape, dtype, name=name, tag=tag, align_bytes=64)
+
+        def in_bank(shape, name, number):
+            return psum.tile(shape, F32, name=name, tag="bank_%d" % number)
 
         x_plane = held([P, PASSES, T], U8, "x_plane")
         nc.gpsimd.memset(x_plane[:].rearrange("p z c -> p (z c)").bitcast(I32), 0)
@@ -59,14 +67,13 @@ def tile_picked_wlapl_none_l_kernel(tc, x_words, x_scales, w1, w2, gate, pos1, p
             x_codes.append(codes)
         lists = []
         for d, pos in enumerate((pos1, pos2)):
-            offsets = keep.tile([P, T // 16], U16, name="offsets_%d" % d)
+            offsets = keep.tile([P, T // LIST_ROWS], U16, name="offsets_%d" % d)
             nc.sync.dma_start(offsets[:], pos)
             lists.append(offsets)
-
-        gate_columns = held([P, 2, SPREAD], F32, "gate_columns")
-        nc.sync.dma_start(out=gate_columns[:], in_=gate[:, 0, HALF:T].rearrange("d (p j) -> p d j", j=SPREAD))
+        gate_dealt = held([P, NEIGHBOURS, GATE_RUN], F32, "gate_dealt")
+        nc.sync.dma_start(out=gate_dealt[:], in_=gate[:, 0, HALF:T].rearrange("d (p j) -> p d j", j=GATE_RUN))
         gate_raw = []
-        for d in range(2):
+        for d in range(NEIGHBOURS):
             raw = held([P, HALF], F32, "gate_raw_%d" % d)
             nc.sync.dma_start(out=raw[:], in_=gate[d, :, 0:HALF])
             gate_raw.append(raw)
@@ -80,30 +87,29 @@ def tile_picked_wlapl_none_l_kernel(tc, x_words, x_scales, w1, w2, gate, pos1, p
         identity = held([P, P], F32, "identity")
         make_identity(nc, identity[:])
 
-        def quantise_weights(raw, name, on_vector, tag=None):
-            grouped = held([P, P, PACK], BF16, name + "_grouped", tag)
-            dst = grouped[:].rearrange("p (c i) j -> p c j i", i=4)
-            src = raw[:].rearrange("p j (c i) -> p c j i", i=4)
-            if on_vector:
-                nc.vector.tensor_copy(out=dst, in_=src)
-            else:
-                nc.scalar.copy(out=dst, in_=src)
-            codes = held([P, P], U32, name + "_codes")
-            plane = held([P, P], U8, name + "_plane")
-            nc.vector.quantize_mx(out=codes[:].bitcast(FP8X4), scales=plane[:], in_=grouped[:].rearrange("p c j -> p (c j)"))
-            return codes, plane
+        def quantise_weights(raws, name, copy, slot=None):
+            width = len(raws) * P
+            grouped = held([P, width * PACK], BF16, name + "_grouped", slot)
+            for n, raw in enumerate(raws):
+                copy(
+                    out=grouped[:, n * K_PASS : (n + 1) * K_PASS].rearrange("p (c i j) -> p c j i", i=RUN, j=PACK),
+                    in_=raw[:].rearrange("p j (c i) -> p c j i", i=RUN),
+                )
+            codes = held([P, width], U32, name + "_codes")
+            plane = held([P, width], U8, name + "_plane")
+            nc.vector.quantize_mx(out=codes[:].bitcast(FP8X4), scales=plane[:], in_=grouped[:])
+            return [(codes[:, n * P : (n + 1) * P], plane[:, n * P : (n + 1) * P]) for n in range(len(raws))]
 
-        def project(c):
-            weights = [quantise_weights(w1_raw[c, z], "w1_%d_%d" % (c, z), 2 * c + z <= 2, "slot_%d" % (2 * c + z)) for z in range(PASSES)]
+        def project(c, weights):
             h_tile = held([P, T], F32, "h_%d" % c)
-            banks = [psum.tile([P, BANK], F32, name="h_bank", tag="bank_%d" % n) for n in range(T // BANK)]
+            banks = [in_bank([P, BANK], "h_bank", n) for n in range(T // BANK)]
             for z in range(PASSES):
                 codes, plane = weights[z]
                 for n, bank in enumerate(banks):
                     nc.tensor.matmul_mx(
                         out=bank[:],
-                        lhsT=codes[:].bitcast(FP8X4),
-                        lhsT_scale=plane[:],
+                        lhsT=codes.bitcast(FP8X4),
+                        lhsT_scale=plane,
                         rhs=x_codes[z][:, 2 * n * BANK : 2 * (n + 1) * BANK].bitcast(FP4X4),
                         rhs_scale=x_plane[:, z, n * BANK : (n + 1) * BANK],
                         start=(z == 0),
@@ -113,75 +119,87 @@ def tile_picked_wlapl_none_l_kernel(tc, x_words, x_scales, w1, w2, gate, pos1, p
                 nc.scalar.copy(out=h_tile[:, n * BANK : (n + 1) * BANK], in_=bank[:])
             return h_tile
 
-        minus_gate = [held([P, T], F32, "minus_gate_%d" % d) for d in range(2)]
+        minus_gate = [held([P, T], F32, "minus_gate_%d" % d) for d in range(NEIGHBOURS)]
 
         def negate_gate(d):
             nc.vector.tensor_scalar_mul(minus_gate[d][:, 0:HALF], gate_raw[d][:], -1.0)
-
-        def spread_gate(d):
-            repeated = held([P, SPREAD, P], F32, "gate_repeated_%d" % d)
-            nc.vector.tensor_scalar_mul(repeated[:], gate_columns[:, d, :].unsqueeze(2).to_broadcast([P, SPREAD, P]), -1.0)
-            bank = psum.tile([P, SPREAD, P], F32, name="gate_bank", tag="bank_%d" % d)
-            for j in range(SPREAD):
+            repeated = held([P, GATE_RUN, P], F32, "gate_repeated_%d" % d)
+            nc.vector.tensor_scalar_mul(repeated[:], gate_dealt[:, d, :].unsqueeze(2).to_broadcast([P, GATE_RUN, P]), -1.0)
+            bank = in_bank([P, GATE_RUN, P], "gate_bank", d)
+            for j in range(GATE_RUN):
                 nc.tensor.transpose(bank[:, j, :], repeated[:, j, :], identity[:])
             nc.scalar.copy(
-                out=minus_gate[d][:, HALF:T].rearrange("p (n j) -> p n j", j=SPREAD), in_=bank[:].rearrange("p j n -> p n j")
+                out=minus_gate[d][:, HALF:T].rearrange("p (n j) -> p n j", j=GATE_RUN), in_=bank[:].rearrange("p j n -> p n j")
             )
 
-        rounded = [held([P, HALF * PACK], BF16, "rounded_%d" % half) for half in range(2)]
+        rounded = [held([P, (HALF // P) * H], BF16, "rounded_%d" % half) for half in range(T // HALF)]
 
-        def look_up(c, d, v0, term):
-            width = term.shape[1]
-            nc.vector.tensor_tensor(
-                term, h[c][:].indirect(lists[d][:, v0 // 16 : (v0 + width) // 16]), minus_gate[d][:, v0 : v0 + width], MULT
-            )
+        def rounded_from(v0):
+            half, start = divmod(v0, HALF)
+            return rounded[half][:].rearrange("v (b u p e) -> v b u p e", u=2, p=P, e=2)[:, start // P :]
+
+        def term_tiles(name, slots):
+            return [held([P, HALF], F32, "%s_%d" % (name, d), slots[d])[:] for d in range(NEIGHBOURS)]
+
+        def term_slices(name, count, width, slot):
+            tile = held([P, count * width], F32, name, slot)
+            return [tile[:, i * width : (i + 1) * width] for i in range(count)]
+
+        def look_up(c, v0, terms):
+            width = terms[0].shape[1]
+            for d in range(NEIGHBOURS):
+                offsets = lists[d][:, v0 // LIST_ROWS : (v0 + width) // LIST_ROWS]
+                nc.vector.tensor_tensor(terms[d], h[c][:].indirect(offsets), minus_gate[d][:, v0 : v0 + width], MULT)
+            return h[c][:, v0 : v0 + width], terms[0], terms[1]
 
         def add_turned(target, part, i):
-            nc.tensor.matmul(target, part, identity[:], start=(i == 0), stop=(i == 2), is_transpose=True)
+            nc.tensor.matmul(target, part, identity[:], start=(i == 0), stop=(i == NEIGHBOURS), is_transpose=True)
 
-        def rounded_view(v0):
-            half, g0 = divmod(v0, HALF)
-            return rounded[half][:].rearrange("v (b u p e) -> v b u p e", u=2, p=P, e=2)[:, g0 // P :]
-
-        def first_tile(v0, slots, bank_tag):
-            terms = [held([P, HALF], F32, "term_first_%d_%d" % (v0, d), "slot_%d" % slots[d]) for d in range(2)]
-            for d in range(2):
-                look_up(0, d, v0, terms[d][:])
-            bank = psum.tile([P, HALF], F32, name="first_bank", tag=bank_tag)
+        def first_tile(v0, slots, bank_number):
+            parts = look_up(0, v0, term_tiles("term_first_%d" % v0, slots))
+            bank = in_bank([P, HALF], "first_bank", bank_number)
             for b in range(HALF // P):
-                cols = slice(b * P, (b + 1) * P)
-                for i, part in enumerate((h[0][:, v0 : v0 + HALF], terms[0], terms[1])):
-                    add_turned(bank[:, cols], part[:, cols], i)
-            return bank, terms
+                for i, part in enumerate(parts):
+                    add_turned(bank[:, b * P : (b + 1) * P], part[:, b * P : (b + 1) * P], i)
+            return bank
 
         def round_first(v0, bank):
-            nc.scalar.copy(out=rounded_view(v0)[:, :, :, 0:32, :], in_=bank[:].rearrange("v (b p u e) -> v b u p e", p=32, u=2, e=2))
+            nc.scalar.copy(
+                out=rounded_from(v0)[:, :, :, 0:TILE_WORDS, :],
+                in_=bank[:].rearrange("v (b p u e) -> v b u p e", p=TILE_WORDS, u=2, e=2),
+            )
+
+        def block_banks(numbers):
+            return [in_bank([P, H - P], "z_bank", n) for n in numbers]
 
         def later_tile(c, v0, terms, z_banks):
-            width = len(z_banks) * P
-            for d in range(2):
-                look_up(c, d, v0, terms[d])
-            for i, part in enumerate((h[c][:, v0 : v0 + width], terms[0], terms[1])):
+            for i, part in enumerate(look_up(c, v0, terms)):
                 for b, bank in enumerate(z_banks):
                     add_turned(bank[:, (c - 1) * P : c * P], part[:, b * P : (b + 1) * P], i)
 
         def round_block(v0, bank, c0, c1):
             nc.scalar.copy(
-                out=rounded_view(v0)[:, 0, :, 32 * c0 : 32 * c1, :],
+                out=rounded_from(v0)[:, 0, :, TILE_WORDS * c0 : TILE_WORDS * c1, :],
                 in_=bank[:, (c0 - 1) * P : (c1 - 1) * P].rearrange("v (p u e) -> v u p e", u=2, e=2),
             )
 
-        def quantise_z(v0, blocks, copy_words, bank_tag, slot):
+        def late_chunk(v0, z_banks, terms):
+            for c in range(1, TILES):
+                later_tile(c, v0, terms[NEIGHBOURS * (c - 1) : NEIGHBOURS * c], z_banks)
+            for b, bank in enumerate(z_banks):
+                round_block(v0 + b * P, bank, 1, TILES)
+
+        def quantise_z(v0, blocks, bank_number, slot=None):
             width = blocks * P
-            half, g0 = divmod(v0, HALF)
-            turned = psum.tile([P, blocks, 2, P], F32, name="turned", tag=bank_tag)
+            half, start = divmod(v0, HALF)
+            turned = in_bank([P, blocks, 2, P], "turned", bank_number)
             words = rounded[half][:].bitcast(F32)
             for b in range(blocks):
                 for u in range(2):
-                    w0 = 2 * (g0 + b * P) + u * P
-                    nc.tensor.transpose(turned[:, b, u, :], words[:, w0 : w0 + P], identity[:])
+                    first_word = 2 * (start + b * P) + u * P
+                    nc.tensor.transpose(turned[:, b, u, :], words[:, first_word : first_word + P], identity[:])
             grouped = held([P, width * PACK], BF16, "z_grouped_%d" % v0, slot)
-            copy_words(
+            nc.scalar.copy(
                 out=grouped[:].bitcast(F32).rearrange("p (b v u) -> p b v u", b=blocks, u=2),
                 in_=turned[:].rearrange("p b u v -> p b v u"),
             )
@@ -190,76 +208,65 @@ def tile_picked_wlapl_none_l_kernel(tc, x_words, x_scales, w1, w2, gate, pos1, p
             nc.vector.quantize_mx(out=codes[:].bitcast(FP8X4), scales=plane[:], in_=grouped[:])
             return v0, width, codes, plane
 
-        def project_out(quantised, copy_out, bank_tag):
+        def project_out(quantised, copy, bank_number):
             v0, width, codes, plane = quantised
-            bank = psum.tile([P, width], F32, name="out_bank", tag=bank_tag)
+            bank = in_bank([P, width], "out_bank", bank_number)
             nc.tensor.matmul_mx(
                 out=bank[:],
-                lhsT=w2_codes[:].bitcast(FP8X4),
-                lhsT_scale=w2_plane[:],
+                lhsT=w2_codes.bitcast(FP8X4),
+                lhsT_scale=w2_plane,
                 rhs=codes[:].bitcast(FP8X4),
                 rhs_scale=plane[:],
                 start=True,
                 stop=True,
             )
             result = held([P, width], F32, "result_%d" % v0)
-            copy_out(out=result[:], in_=bank[:])
+            copy(out=result[:], in_=bank[:])
             nc.sync.dma_start(out=out[:, v0 : v0 + width], in_=result[:])
 
-        def new_banks(numbers):
-            return [psum.tile([P, H - P], F32, name="z_bank", tag="bank_%d" % n) for n in numbers]
-
-        def late_chunk(v0, z_banks, terms):
-            width = len(z_banks) * P
-            for c in range(1, TILES):
-                pair = terms[2 * (c - 1) : 2 * c]
-                later_tile(c, v0, pair, z_banks)
-                if v0 + width == T and c >= TILES - 2:
-                    round_block(v0, z_banks[0], 1 if c == TILES - 2 else c, c + 1)
-            if v0 + width < T:
-                for b, bank in enumerate(z_banks):
-                    round_block(v0 + b * P, bank, 1, TILES)
-            return pair[1]
-
-        def term_slices(name, count, width, slot):
-            tile = held([P, count * width], F32, name, slot)
-            return [tile[:, i * width : (i + 1) * width] for i in range(count)]
-
-        h = [project(0)]
-        for d in range(2):
+        h = [project(0, [quantise_weights([w1_raw[0, z]], "w1_0_%d" % z, on_vector, z)[0] for z in range(PASSES)])]
+        for d in range(NEIGHBOURS):
             negate_gate(d)
-            spread_gate(d)
-        h.append(project(1))
-        bank0, clock0 = first_tile(0, (0, 3), "bank_2")
-        h.append(project(2))
-        bank1, clock1 = first_tile(HALF, (1, 5), "bank_3")
-        h.append(project(3))
-        round_first(0, bank0)
-        round_first(HALF, bank1)
-        w2_codes, w2_plane = quantise_weights(w2_raw, "w2", False)
+        h.append(
+            project(1, quantise_weights([w1_raw[1, 0]], "w1_1_0", on_vector, 2) + quantise_weights([w1_raw[1, 1]], "w1_1_1", on_scalar, 3))
+        )
+        first_low = first_tile(0, (0, 3), 2)
+        h.append(project(2, quantise_weights([w1_raw[2, z] for z in range(PASSES)], "w1_2", on_scalar, 5)))
+        first_high = first_tile(HALF, (1, 5), 3)
+        h.append(project(3, quantise_weights([w1_raw[3, z] for z in range(PASSES)], "w1_3", on_scalar, 7)))
+        round_first(0, first_low)
+        round_first(HALF, first_high)
+        w2_codes, w2_plane = quantise_weights([w2_raw], "w2", on_scalar)[0]
 
-        z_banks = new_banks((4, 5, 6, 7))
+        z_banks = block_banks((4, 5, 6, 7))
         for c, slots in ((1, (6, 7)), (2, (2, 4)), (3, (0, 1))):
-            terms = [held([P, HALF], F32, "term_%d_%d" % (c, d), "slot_%d" % slots[d]) for d in range(2)]
-            later_tile(c, 0, [term[:] for term in terms], z_banks)
+            later_tile(c, 0, term_tiles("term_%d" % c, slots), z_banks)
         for b in range(2):
             round_block(b * P, z_banks[b], 1, TILES)
-        first = quantise_z(0, 2, nc.scalar.copy, "bank_2", "slot_3")
+        z_01 = quantise_z(0, 2, 2, 3)
         for b in range(2, 4):
             round_block(b * P, z_banks[b], 1, TILES)
-        second = quantise_z(2 * P, 2, nc.scalar.copy, "bank_3", None)
-        late_chunk(4 * P, new_banks((4, 5)), term_slices("third_a", 3, 2 * P, "slot_2") + term_slices("third_b", 3, 2 * P, "slot_4"))
-        project_out(first, nc.scalar.copy, "bank_4")
-        third = quantise_z(4 * P, 2, nc.scalar.copy, "bank_6", None)
-        closing_terms = term_slices("closing", 7, P, "slot_3")
-        late_chunk(6 * P, new_banks((3,)), term_slices("fourth", 5, P, "slot_1") + closing_terms[:1])
-        fourth = quantise_z(6 * P, 1, nc.scalar.copy, "bank_2", None)
-        closing = late_chunk(7 * P, new_banks((5,)), closing_terms[1:])
-        last = True
-        if last:
-            pass
-        fifth = quantise_z(7 * P, 1, nc.scalar.copy, "bank_7", None)
-        project_out(second, nc.vector.tensor_copy, "bank_2")
-        project_out(third, nc.vector.tensor_copy, "bank_5")
-        project_out(fourth, nc.vector.tensor_copy, "bank_7")
-        project_out(fifth, nc.scalar.copy, "bank_0")
+        z_23 = quantise_z(2 * P, 2, 3)
+
+        late_terms = NEIGHBOURS * (TILES - 1)
+        late_chunk(
+            4 * P,
+            block_banks((4, 5)),
+            term_slices("terms_45_low", late_terms // 2, 2 * P, 2) + term_slices("terms_45_high", late_terms // 2, 2 * P, 4),
+        )
+        project_out(z_01, on_scalar, 4)
+        z_45 = quantise_z(4 * P, 2, 6)
+        closing = term_slices("terms_closing", 1 + late_terms, P, 3)
+        late_chunk(6 * P, block_banks((3,)), term_slices("terms_6", late_terms - 1, P, 1) + closing[:1])
+        z_6 = quantise_z(6 * P, 1, 2)
+        z_banks = block_banks((5,))
+        for c in range(1, TILES):
+            later_tile(c, 7 * P, closing[1 + NEIGHBOURS * (c - 1) : 1 + NEIGHBOURS * c], z_banks)
+            if c == TILES - 2:
+                round_block(7 * P, z_banks[0], 1, TILES - 1)
+        round_block(7 * P, z_banks[0], TILES - 1, TILES)
+        z_7 = quantise_z(7 * P, 1, 7)
+        project_out(z_23, on_vector, 2)
+        project_out(z_45, on_vector, 5)
+        project_out(z_6, on_vector, 7)
+        project_out(z_7, on_scalar, 0)

from contextlib import ExitStack

import concourse.mybir as mybir
from concourse.masks import make_identity

K, T, H, N = 1024, 1024, 512, 128
FLOPS = 2 * K * H * T + 2 * H * N * T

F32 = mybir.dt.float32
BF16 = mybir.dt.bfloat16
I32 = mybir.dt.int32
U32 = mybir.dt.uint32
U16 = mybir.dt.uint16
U8 = mybir.dt.uint8
FP8X4 = mybir.dt.float8_e4m3fn_x4
FP4X4 = mybir.dt.float4_e2m1fn_x4
MULT = mybir.AluOpType.mult

P = 128
PACK = 4
K_PASS = P * PACK
PASSES = K // K_PASS
TILES = H // P
TILE_WORDS = P // PACK
BANK = 512
HALF = T // 2
GATE_RUN = HALF // P
LIST_ROWS = 16
NEIGHBOURS = 2
RUN = 4


def tile_picked_wlapl_none_l_kernel(tc, x_words, x_scales, w1, w2, gate, pos1, pos2, out):
    nc = tc.nc
    on_vector, on_scalar = nc.vector.tensor_copy, nc.scalar.copy
    with ExitStack() as ctx:
        keep = ctx.enter_context(tc.tile_pool(name="keep", bufs=1))
        psum = ctx.enter_context(tc.psum_pool(name="psum", bufs=1))

        def held(shape, dtype, name, slot=None):
            tag = name if slot is None else "slot_%d" % slot
            return keep.tile(shape, dtype, name=name, tag=tag, align_bytes=64)

        def in_bank(shape, name, number):
            return psum.tile(shape, F32, name=name, tag="bank_%d" % number)

        x_plane = held([P, PASSES, T], U8, "x_plane")
        nc.gpsimd.memset(x_plane[:].rearrange("p z c -> p (z c)").bitcast(I32), 0)

        def load_w1(c, z):
            raw = held([P, PACK, P], F32, "w1_raw_%d_%d" % (c, z))
            rows = w1[z * K_PASS : (z + 1) * K_PASS, c * P : (c + 1) * P]
            nc.sync.dma_start(out=raw[:], in_=rows.rearrange("(p j) n -> p j n", j=PACK))
            return raw

        for q in range(4):
            nc.sync.dma_start(
                out=x_plane[32 * q : 32 * q + 4].bitcast(I32),
                in_=x_scales[:, 4 * q : 4 * q + 4, :].rearrange("z r c -> r z c").bitcast(I32),
            )
        w1_raw = {}
        x_codes = []
        for z in range(PASSES):
            w1_raw[0, z] = load_w1(0, z)
            codes = held([P, 2 * T], U8, "x_codes_%d" % z)
            nc.sync.dma_start(out=codes[:], in_=x_words[z])
            x_codes.append(codes)
        lists = []
        for d, pos in enumerate((pos1, pos2)):
            offsets = keep.tile([P, T // LIST_ROWS], U16, name="offsets_%d" % d)
            nc.sync.dma_start(offsets[:], pos)
            lists.append(offsets)
        gate_dealt = held([P, NEIGHBOURS, GATE_RUN], F32, "gate_dealt")
        nc.sync.dma_start(out=gate_dealt[:], in_=gate[:, 0, HALF:T].rearrange("d (p j) -> p d j", j=GATE_RUN))
        gate_raw = []
        for d in range(NEIGHBOURS):
            raw = held([P, HALF], F32, "gate_raw_%d" % d)
            nc.sync.dma_start(out=raw[:], in_=gate[d, :, 0:HALF])
            gate_raw.append(raw)
            w1_raw[1, d] = load_w1(1, d)
        for c in range(2, TILES):
            for z in range(PASSES):
                w1_raw[c, z] = load_w1(c, z)
        w2_raw = held([P, PACK, N], F32, "w2_raw")
        nc.sync.dma_start(out=w2_raw[:], in_=w2.rearrange("(p j) n -> p j n", j=PACK))

        identity = held([P, P], F32, "identity")
        make_identity(nc, identity[:])

        def quantise_weights(raws, name, copy, slot=None):
            width = len(raws) * P
            grouped = held([P, width * PACK], BF16, name + "_grouped", slot)
            for n, raw in enumerate(raws):
                copy(
                    out=grouped[:, n * K_PASS : (n + 1) * K_PASS].rearrange("p (c i j) -> p c j i", i=RUN, j=PACK),
                    in_=raw[:].rearrange("p j (c i) -> p c j i", i=RUN),
                )
            codes = held([P, width], U32, name + "_codes")
            plane = held([P, width], U8, name + "_plane")
            nc.vector.quantize_mx(out=codes[:].bitcast(FP8X4), scales=plane[:], in_=grouped[:])
            return [(codes[:, n * P : (n + 1) * P], plane[:, n * P : (n + 1) * P]) for n in range(len(raws))]

        def project(c, weights):
            h_tile = held([P, T], F32, "h_%d" % c)
            banks = [in_bank([P, BANK], "h_bank", n) for n in range(T // BANK)]
            for z in range(PASSES):
                codes, plane = weights[z]
                for n, bank in enumerate(banks):
                    nc.tensor.matmul_mx(
                        out=bank[:],
                        lhsT=codes.bitcast(FP8X4),
                        lhsT_scale=plane,
                        rhs=x_codes[z][:, 2 * n * BANK : 2 * (n + 1) * BANK].bitcast(FP4X4),
                        rhs_scale=x_plane[:, z, n * BANK : (n + 1) * BANK],
                        start=(z == 0),
                        stop=(z == PASSES - 1),
                    )
            for n, bank in enumerate(banks):
                nc.scalar.copy(out=h_tile[:, n * BANK : (n + 1) * BANK], in_=bank[:])
            return h_tile

        minus_gate = [held([P, T], F32, "minus_gate_%d" % d) for d in range(NEIGHBOURS)]

        def negate_gate(d):
            nc.vector.tensor_scalar_mul(minus_gate[d][:, 0:HALF], gate_raw[d][:], -1.0)
            repeated = held([P, GATE_RUN, P], F32, "gate_repeated_%d" % d)
            nc.vector.tensor_scalar_mul(repeated[:], gate_dealt[:, d, :].unsqueeze(2).to_broadcast([P, GATE_RUN, P]), -1.0)
            bank = in_bank([P, GATE_RUN, P], "gate_bank", d)
            for j in range(GATE_RUN):
                nc.tensor.transpose(bank[:, j, :], repeated[:, j, :], identity[:])
            nc.scalar.copy(
                out=minus_gate[d][:, HALF:T].rearrange("p (n j) -> p n j", j=GATE_RUN), in_=bank[:].rearrange("p j n -> p n j")
            )

        rounded = [held([P, (HALF // P) * H], BF16, "rounded_%d" % half) for half in range(T // HALF)]

        def rounded_from(v0):
            half, start = divmod(v0, HALF)
            return rounded[half][:].rearrange("v (b u p e) -> v b u p e", u=2, p=P, e=2)[:, start // P :]

        def term_tiles(name, slots):
            return [held([P, HALF], F32, "%s_%d" % (name, d), slots[d])[:] for d in range(NEIGHBOURS)]

        def term_slices(name, count, width, slot):
            tile = held([P, count * width], F32, name, slot)
            return [tile[:, i * width : (i + 1) * width] for i in range(count)]

        def look_up(c, v0, terms):
            width = terms[0].shape[1]
            for d in range(NEIGHBOURS):
                offsets = lists[d][:, v0 // LIST_ROWS : (v0 + width) // LIST_ROWS]
                nc.vector.tensor_tensor(terms[d], h[c][:].indirect(offsets), minus_gate[d][:, v0 : v0 + width], MULT)
            return h[c][:, v0 : v0 + width], terms[0], terms[1]

        def add_turned(target, part, i):
            nc.tensor.matmul(target, part, identity[:], start=(i == 0), stop=(i == NEIGHBOURS), is_transpose=True)

        def first_tile(v0, slots, bank_number):
            parts = look_up(0, v0, term_tiles("term_first_%d" % v0, slots))
            bank = in_bank([P, HALF], "first_bank", bank_number)
            for b in range(HALF // P):
                for i, part in enumerate(parts):
                    add_turned(bank[:, b * P : (b + 1) * P], part[:, b * P : (b + 1) * P], i)
            return bank

        def round_first(v0, bank):
            nc.scalar.copy(
                out=rounded_from(v0)[:, :, :, 0:TILE_WORDS, :],
                in_=bank[:].rearrange("v (b p u e) -> v b u p e", p=TILE_WORDS, u=2, e=2),
            )

        def block_banks(numbers):
            return [in_bank([P, H - P], "z_bank", n) for n in numbers]

        def later_tile(c, v0, terms, z_banks):
            for i, part in enumerate(look_up(c, v0, terms)):
                for b, bank in enumerate(z_banks):
                    add_turned(bank[:, (c - 1) * P : c * P], part[:, b * P : (b + 1) * P], i)

        def round_block(v0, bank, c0, c1):
            nc.scalar.copy(
                out=rounded_from(v0)[:, 0, :, TILE_WORDS * c0 : TILE_WORDS * c1, :],
                in_=bank[:, (c0 - 1) * P : (c1 - 1) * P].rearrange("v (p u e) -> v u p e", u=2, e=2),
            )

        def late_chunk(v0, z_banks, terms):
            for c in range(1, TILES):
                later_tile(c, v0, terms[NEIGHBOURS * (c - 1) : NEIGHBOURS * c], z_banks)
            for b, bank in enumerate(z_banks):
                round_block(v0 + b * P, bank, 1, TILES)

        def quantise_z(v0, blocks, bank_number, slot=None):
            width = blocks * P
            half, start = divmod(v0, HALF)
            turned = in_bank([P, blocks, 2, P], "turned", bank_number)
            words = rounded[half][:].bitcast(F32)
            for b in range(blocks):
                for u in range(2):
                    first_word = 2 * (start + b * P) + u * P
                    nc.tensor.transpose(turned[:, b, u, :], words[:, first_word : first_word + P], identity[:])
            grouped = held([P, width * PACK], BF16, "z_grouped_%d" % v0, slot)
            nc.scalar.copy(
                out=grouped[:].bitcast(F32).rearrange("p (b v u) -> p b v u", b=blocks, u=2),
                in_=turned[:].rearrange("p b u v -> p b v u"),
            )
            codes = held([P, width], U32, "z_codes_%d" % v0)
            plane = held([P, width], U8, "z_plane_%d" % v0)
            nc.vector.quantize_mx(out=codes[:].bitcast(FP8X4), scales=plane[:], in_=grouped[:])
            return v0, width, codes, plane

        def project_out(quantised, copy, bank_number):
            v0, width, codes, plane = quantised
            bank = in_bank([P, width], "out_bank", bank_number)
            nc.tensor.matmul_mx(
                out=bank[:],
                lhsT=w2_codes.bitcast(FP8X4),
                lhsT_scale=w2_plane,
                rhs=codes[:].bitcast(FP8X4),
                rhs_scale=plane[:],
                start=True,
                stop=True,
            )
            result = held([P, width], F32, "result_%d" % v0)
            copy(out=result[:], in_=bank[:])
            nc.sync.dma_start(out=out[:, v0 : v0 + width], in_=result[:])

        h = [project(0, [quantise_weights([w1_raw[0, z]], "w1_0_%d" % z, on_vector, z)[0] for z in range(PASSES)])]
        for d in range(NEIGHBOURS):
            negate_gate(d)
        h.append(
            project(1, quantise_weights([w1_raw[1, 0]], "w1_1_0", on_vector, 2) + quantise_weights([w1_raw[1, 1]], "w1_1_1", on_scalar, 3))
        )
        first_low = first_tile(0, (0, 3), 2)
        h.append(project(2, quantise_weights([w1_raw[2, z] for z in range(PASSES)], "w1_2", on_scalar, 5)))
        first_high = first_tile(HALF, (1, 5), 3)
        h.append(project(3, quantise_weights([w1_raw[3, z] for z in range(PASSES)], "w1_3", on_scalar, 7)))
        round_first(0, first_low)
        round_first(HALF, first_high)
        w2_codes, w2_plane = quantise_weights([w2_raw], "w2", on_scalar)[0]

        z_banks = block_banks((4, 5, 6, 7))
        for c, slots in ((1, (6, 7)), (2, (2, 4)), (3, (0, 1))):
            later_tile(c, 0, term_tiles("term_%d" % c, slots), z_banks)
        for b in range(2):
            round_block(b * P, z_banks[b], 1, TILES)
        z_01 = quantise_z(0, 2, 2, 3)
        for b in range(2, 4):
            round_block(b * P, z_banks[b], 1, TILES)
        z_23 = quantise_z(2 * P, 2, 3)

        late_terms = NEIGHBOURS * (TILES - 1)
        late_chunk(
            4 * P,
            block_banks((4, 5)),
            term_slices("terms_45_low", late_terms // 2, 2 * P, 2) + term_slices("terms_45_high", late_terms // 2, 2 * P, 4),
        )
        project_out(z_01, on_scalar, 4)
        z_45 = quantise_z(4 * P, 2, 6)
        closing = term_slices("terms_closing", 1 + late_terms, P, 3)
        late_chunk(6 * P, block_banks((3,)), term_slices("terms_6", late_terms - 1, P, 1) + closing[:1])
        z_6 = quantise_z(6 * P, 1, 2)
        z_banks = block_banks((5,))
        for c in range(1, TILES):
            later_tile(c, 7 * P, closing[1 + NEIGHBOURS * (c - 1) : 1 + NEIGHBOURS * c], z_banks)
            if c == TILES - 2:
                round_block(7 * P, z_banks[0], 1, TILES - 1)
        round_block(7 * P, z_banks[0], TILES - 1, TILES)
        z_7 = quantise_z(7 * P, 1, 7)
        project_out(z_23, on_vector, 2)
        project_out(z_45, on_vector, 5)
        project_out(z_6, on_vector, 7)
        project_out(z_7, on_scalar, 0)
